import numpy as np
import ml_dtypes

BF16 = ml_dtypes.bfloat16


def bf(x):
    return np.asarray(x, np.float32).astype(BF16)


def f32(x):
    return np.asarray(x, np.float32)


def f64(x):
    return np.asarray(x).astype(np.float64)


def striped(idx):
    return np.tile(idx.reshape(-1, 16).T, (8, 1))


S, K, H, M, N, E, Q = 512, 256, 256, 256, 192, 1, 192


def setup_inputs():
    return {"base": bf(np.random.standard_normal((M, S))), "x": bf(np.random.standard_normal((K, N))), "w": bf(np.random.standard_normal((E, K, H)) / np.sqrt(K)), "b": f32(0.5 * np.random.standard_normal((H, E))), "w2": bf(1.5 * np.random.standard_normal((E, H, M)) / np.sqrt(H)), "c": f32(0.2 + 0.8 * np.random.random_sample((1, N))), "offs": striped(np.random.permutation(S)[:N])}


def reference(base, x, w, b, w2, c, offs):
    idx = offs[:16].T.reshape(-1)
    z = f64(base).copy()
    for e in range(E):
        t = f64(w)[e].T @ f64(x)[:, e * Q : (e + 1) * Q] + f64(b)[:, e : e + 1]
        t = np.maximum(t, 0.0) * f64(c)[:, e * Q : (e + 1) * Q]
        z[:, idx[e * Q : (e + 1) * Q]] += f64(w2)[e].T @ t
    return z

@@ -1,0 +1,73 @@
+import concourse.mybir as mybir
+from concourse.masks import make_identity
+
+P = 128
+S, K, H, M, N = 512, 256, 256, 256, 192
+BF16, F32, U16 = mybir.dt.bfloat16, mybir.dt.float32, mybir.dt.uint16
+MAX, MULT = mybir.AluOpType.max, mybir.AluOpType.mult
+
+FLOPS = 2 * N * (K * H + H * M)
+
+
+def tile_rows_ffnback_relu_kernel(tc, base, x, w, b, w2, c, offs, out):
+    nc = tc.nc
+    with (
+        tc.tile_pool(name="held", bufs=1) as held,
+        tc.psum_pool(name="psum", bufs=1) as psum,
+    ):
+        x_tile = held.tile([P, K // P, N], BF16)
+        nc.sync.dma_start(x_tile[:], x.rearrange("(a p) n -> p a n", p=P))
+        w_tile = held.tile([P, K // P, H], BF16)
+        nc.sync.dma_start(w_tile[:], w.rearrange("e (a p) h -> p (e a) h", p=P))
+        base_tile = held.tile([P, M // P, S], BF16)
+        nc.sync.dma_start(base_tile[:], base.rearrange("(a p) s -> p a s", p=P))
+        w2_tile = held.tile([P, H // P, M], BF16)
+        nc.sync.dma_start(w2_tile[:], w2.rearrange("e (a p) m -> p (e a) m", p=P))
+        offsets = held.tile([P, N // 16], U16)
+        nc.sync.dma_start(offsets[:], offs)
+
+        c_row = held.tile([1, N], F32)
+        nc.scalar.dma_start(c_row[:], c)
+        b_row = held.tile([1, H], F32)
+        nc.scalar.dma_start(b_row[:], b.rearrange("h e -> e h"))
+
+        ones_row = held.tile([1, N], F32)
+        nc.vector.memset(ones_row[:], 1.0)
+        ident = held.tile([P, P], BF16)
+        make_identity(nc, ident[:])
+
+        c_bank = psum.tile([P, N], F32)
+        nc.tensor.matmul(c_bank[:], ones_row[:, :P], c_row[:], start=True, stop=True)
+        c_all = held.tile([P, N], F32)
+        nc.vector.tensor_copy(c_all[:], c_bank[:])
+
+        sums = [psum.tile([P, N], F32, name=f"sums{i}") for i in range(H // P)]
+        for i in range(H // P):
+            rows = slice(i * P, (i + 1) * P)
+            nc.tensor.matmul(sums[i][:], b_row[:, rows], ones_row[:], start=True, stop=False)
+            for k in range(K // P):
+                nc.tensor.matmul(sums[i][:], w_tile[:, k, rows], x_tile[:, k, :], start=False, stop=k == K // P - 1)
+
+        hidden = [held.tile([P, N], BF16, name=f"hidden{i}") for i in range(H // P)]
+        for i in range(H // P):
+            nc.vector.scalar_tensor_tensor(hidden[i][:], sums[i][:], 0.0, c_all[:], op0=MAX, op1=MULT)
+
+        windows = [psum.tile([P, S], F32, name=f"window{m}") for m in range(M // P)]
+        for m in range(M // P):
+            nc.tensor.matmul(windows[m][:], ident[:], base_tile[:, m, :], start=True, stop=False)
+
+        for m in range(M // P):
+            for i in range(H // P):
+                nc.tensor.matmul(
+                    windows[m][:].indirect(offsets[:]),
+                    w2_tile[:, i, m * P : (m + 1) * P],
+                    hidden[i][:],
+                    start=False,
+                    stop=i == H // P - 1,
+                )
+
+        out_tiles = [held.tile([P, S], F32, name=f"out{m}") for m in range(M // P)]
+        nc.scalar.copy(out_tiles[0][:], windows[0][:])
+        nc.scalar.dma_start(out[0:P, :], out_tiles[0][:])
+        nc.vector.tensor_copy(out_tiles[1][:], windows[1][:])
+        nc.sync.dma_start(out[P : 2 * P, :], out_tiles[1][:])

@@ -4,7 +4,9 @@ from concourse.masks import make_identity
 P = 128
 S, K, H, M, N = 512, 256, 256, 256, 192
 BF16, F32, U16 = mybir.dt.bfloat16, mybir.dt.float32, mybir.dt.uint16
-MAX, MULT = mybir.AluOpType.max, mybir.AluOpType.mult
+ADD, MAX, MULT = mybir.AluOpType.add, mybir.AluOpType.max, mybir.AluOpType.mult
+RELU = mybir.ActivationFunctionType.Relu
+WARM_UPS = 4
 
 FLOPS = 2 * N * (K * H + H * M)
 
@@ -26,31 +28,33 @@ def tile_rows_ffnback_relu_kernel(tc, base, x, w, b, w2, c, offs, out):
         offsets = held.tile([P, N // 16], U16)
         nc.sync.dma_start(offsets[:], offs)
 
-        c_row = held.tile([1, N], F32)
-        nc.scalar.dma_start(c_row[:], c)
-        b_row = held.tile([1, H], F32)
-        nc.scalar.dma_start(b_row[:], b.rearrange("h e -> e h"))
+        b_tile = held.tile([P, H // P], F32)
+        nc.scalar.dma_start(b_tile[:], b.rearrange("(a p) e -> p (e a)", p=P))
+        c_all = held.tile([P, N], F32)
+        nc.scalar.dma_start(c_all[:], c.rearrange("e n -> (e n)").partition_broadcast(P))
 
-        ones_row = held.tile([1, N], F32)
-        nc.vector.memset(ones_row[:], 1.0)
         ident = held.tile([P, P], BF16)
         make_identity(nc, ident[:])
 
-        c_bank = psum.tile([P, N], F32)
-        nc.tensor.matmul(c_bank[:], ones_row[:, :P], c_row[:], start=True, stop=True)
-        c_all = held.tile([P, N], F32)
-        nc.vector.tensor_copy(c_all[:], c_bank[:])
+        zeros = held.tile([P, S], BF16)
+        nc.vector.memset(zeros[:], 0.0)
+        unread = psum.tile([P, S], F32)
+        for t in range(WARM_UPS):
+            nc.tensor.matmul(unread[:], zeros[:, :P], zeros[:], start=True, stop=True)
 
         sums = [psum.tile([P, N], F32, name=f"sums{i}") for i in range(H // P)]
         for i in range(H // P):
             rows = slice(i * P, (i + 1) * P)
-            nc.tensor.matmul(sums[i][:], b_row[:, rows], ones_row[:], start=True, stop=False)
             for k in range(K // P):
-                nc.tensor.matmul(sums[i][:], w_tile[:, k, rows], x_tile[:, k, :], start=False, stop=k == K // P - 1)
+                nc.tensor.matmul(sums[i][:], w_tile[:, k, rows], x_tile[:, k, :], start=k == 0, stop=k == K // P - 1)
 
+        relu0 = held.tile([P, N], F32)
+        nc.vector.tensor_scalar(relu0[:], sums[0][:], b_tile[:, 0:1], 0.0, op0=ADD, op1=MAX)
+        relu1 = held.tile([P, N], F32)
+        nc.scalar.activation(relu1[:], sums[1][:], RELU, bias=b_tile[:, 1:2])
         hidden = [held.tile([P, N], BF16, name=f"hidden{i}") for i in range(H // P)]
-        for i in range(H // P):
-            nc.vector.scalar_tensor_tensor(hidden[i][:], sums[i][:], 0.0, c_all[:], op0=MAX, op1=MULT)
+        nc.vector.tensor_tensor(hidden[0][:], relu0[:], c_all[:], MULT)
+        nc.vector.tensor_tensor(hidden[1][:], relu1[:], c_all[:], MULT)
 
         windows = [psum.tile([P, S], F32, name=f"window{m}") for m in range(M // P)]
         for m in range(M // P):

@@ -6,7 +6,7 @@ S, K, H, M, N = 512, 256, 256, 256, 192
 BF16, F32, U16 = mybir.dt.bfloat16, mybir.dt.float32, mybir.dt.uint16
 ADD, MAX, MULT = mybir.AluOpType.add, mybir.AluOpType.max, mybir.AluOpType.mult
 RELU = mybir.ActivationFunctionType.Relu
-WARM_UPS = 4
+WARM_UPS = 3
 
 FLOPS = 2 * N * (K * H + H * M)
 
@@ -17,10 +17,14 @@ def tile_rows_ffnback_relu_kernel(tc, base, x, w, b, w2, c, offs, out):
         tc.tile_pool(name="held", bufs=1) as held,
         tc.psum_pool(name="psum", bufs=1) as psum,
     ):
+        b_row = held.tile([1, H], F32)
+        nc.sync.dma_start(b_row[:], b.rearrange("h e -> e h"))
         x_tile = held.tile([P, K // P, N], BF16)
         nc.sync.dma_start(x_tile[:], x.rearrange("(a p) n -> p a n", p=P))
         w_tile = held.tile([P, K // P, H], BF16)
         nc.sync.dma_start(w_tile[:], w.rearrange("e (a p) h -> p (e a) h", p=P))
+        c_row = held.tile([1, N], F32)
+        nc.sync.dma_start(c_row[:], c)
         base_tile = held.tile([P, M // P, S], BF16)
         nc.sync.dma_start(base_tile[:], base.rearrange("(a p) s -> p a s", p=P))
         w2_tile = held.tile([P, H // P, M], BF16)
@@ -28,33 +32,45 @@ def tile_rows_ffnback_relu_kernel(tc, base, x, w, b, w2, c, offs, out):
         offsets = held.tile([P, N // 16], U16)
         nc.sync.dma_start(offsets[:], offs)
 
-        b_tile = held.tile([P, H // P], F32)
-        nc.scalar.dma_start(b_tile[:], b.rearrange("(a p) e -> p (e a)", p=P))
-        c_all = held.tile([P, N], F32)
-        nc.scalar.dma_start(c_all[:], c.rearrange("e n -> (e n)").partition_broadcast(P))
-
-        ident = held.tile([P, P], BF16)
-        make_identity(nc, ident[:])
+        zero_column = held.tile([P, 1], F32)
+        nc.vector.memset(zero_column[:], 0.0)
+        unread_column = held.tile([P, 1], F32)
+        nc.scalar.activation(unread_column[:], zero_column[:], RELU)
 
         zeros = held.tile([P, S], BF16)
         nc.vector.memset(zeros[:], 0.0)
-        unread = psum.tile([P, S], F32)
+        unread_bank = psum.tile([P, S], F32)
         for t in range(WARM_UPS):
-            nc.tensor.matmul(unread[:], zeros[:, :P], zeros[:], start=True, stop=True)
+            nc.tensor.matmul(unread_bank[:], zeros[:, :P], zeros[:], start=True, stop=True)
+
+        ones_row = held.tile([1, P], F32)
+        nc.vector.memset(ones_row[:], 1.0)
+        ident = held.tile([P, P], BF16)
+        make_identity(nc, ident[:])
+
+        b_bank = psum.tile([P, H // P], F32)
+        for i in range(H // P):
+            nc.tensor.matmul(b_bank[:, i : i + 1], b_row[:, i * P : (i + 1) * P], ones_row[:, :1], start=True, stop=True)
+        b_tile = held.tile([P, H // P], F32)
+        nc.vector.tensor_copy(b_tile[:], b_bank[:])
 
         sums = [psum.tile([P, N], F32, name=f"sums{i}") for i in range(H // P)]
         for i in range(H // P):
-            rows = slice(i * P, (i + 1) * P)
             for k in range(K // P):
-                nc.tensor.matmul(sums[i][:], w_tile[:, k, rows], x_tile[:, k, :], start=k == 0, stop=k == K // P - 1)
+                nc.tensor.matmul(
+                    sums[i][:], w_tile[:, k, i * P : (i + 1) * P], x_tile[:, k, :], start=k == 0, stop=k == K // P - 1
+                )
+
+        c_bank = psum.tile([P, N], F32)
+        nc.tensor.matmul(c_bank[:], ones_row[:], c_row[:], start=True, stop=True)
 
         relu0 = held.tile([P, N], F32)
         nc.vector.tensor_scalar(relu0[:], sums[0][:], b_tile[:, 0:1], 0.0, op0=ADD, op1=MAX)
         relu1 = held.tile([P, N], F32)
         nc.scalar.activation(relu1[:], sums[1][:], RELU, bias=b_tile[:, 1:2])
         hidden = [held.tile([P, N], BF16, name=f"hidden{i}") for i in range(H // P)]
-        nc.vector.tensor_tensor(hidden[0][:], relu0[:], c_all[:], MULT)
-        nc.vector.tensor_tensor(hidden[1][:], relu1[:], c_all[:], MULT)
+        nc.vector.tensor_tensor(hidden[0][:], relu0[:], c_bank[:], MULT)
+        nc.vector.tensor_tensor(hidden[1][:], relu1[:], c_bank[:], MULT)
 
         windows = [psum.tile([P, S], F32, name=f"window{m}") for m in range(M // P)]
         for m in range(M // P):
@@ -72,6 +88,6 @@ def tile_rows_ffnback_relu_kernel(tc, base, x, w, b, w2, c, offs, out):
 
         out_tiles = [held.tile([P, S], F32, name=f"out{m}") for m in range(M // P)]
         nc.scalar.copy(out_tiles[0][:], windows[0][:])
-        nc.scalar.dma_start(out[0:P, :], out_tiles[0][:])
+        nc.sync.dma_start(out[0:P, :], out_tiles[0][:])
         nc.vector.tensor_copy(out_tiles[1][:], windows[1][:])
         nc.sync.dma_start(out[P : 2 * P, :], out_tiles[1][:])

import concourse.mybir as mybir
from concourse.masks import make_identity

P = 128
S, K, H, M, N = 512, 256, 256, 256, 192
BF16, F32, U16 = mybir.dt.bfloat16, mybir.dt.float32, mybir.dt.uint16
ADD, MAX, MULT = mybir.AluOpType.add, mybir.AluOpType.max, mybir.AluOpType.mult
RELU = mybir.ActivationFunctionType.Relu
WARM_UPS = 3

FLOPS = 2 * N * (K * H + H * M)


def tile_rows_ffnback_relu_kernel(tc, base, x, w, b, w2, c, offs, out):
    nc = tc.nc
    with (
        tc.tile_pool(name="held", bufs=1) as held,
        tc.psum_pool(name="psum", bufs=1) as psum,
    ):
        b_row = held.tile([1, H], F32)
        nc.sync.dma_start(b_row[:], b.rearrange("h e -> e h"))
        x_tile = held.tile([P, K // P, N], BF16)
        nc.sync.dma_start(x_tile[:], x.rearrange("(a p) n -> p a n", p=P))
        w_tile = held.tile([P, K // P, H], BF16)
        nc.sync.dma_start(w_tile[:], w.rearrange("e (a p) h -> p (e a) h", p=P))
        c_row = held.tile([1, N], F32)
        nc.sync.dma_start(c_row[:], c)
        base_tile = held.tile([P, M // P, S], BF16)
        nc.sync.dma_start(base_tile[:], base.rearrange("(a p) s -> p a s", p=P))
        w2_tile = held.tile([P, H // P, M], BF16)
        nc.sync.dma_start(w2_tile[:], w2.rearrange("e (a p) m -> p (e a) m", p=P))
        offsets = held.tile([P, N // 16], U16)
        nc.sync.dma_start(offsets[:], offs)

        zero_column = held.tile([P, 1], F32)
        nc.vector.memset(zero_column[:], 0.0)
        unread_column = held.tile([P, 1], F32)
        nc.scalar.activation(unread_column[:], zero_column[:], RELU)

        zeros = held.tile([P, S], BF16)
        nc.vector.memset(zeros[:], 0.0)
        unread_bank = psum.tile([P, S], F32)
        for t in range(WARM_UPS):
            nc.tensor.matmul(unread_bank[:], zeros[:, :P], zeros[:], start=True, stop=True)

        ones_row = held.tile([1, P], F32)
        nc.vector.memset(ones_row[:], 1.0)
        ident = held.tile([P, P], BF16)
        make_identity(nc, ident[:])

        b_bank = psum.tile([P, H // P], F32)
        for i in range(H // P):
            nc.tensor.matmul(b_bank[:, i : i + 1], b_row[:, i * P : (i + 1) * P], ones_row[:, :1], start=True, stop=True)
        b_tile = held.tile([P, H // P], F32)
        nc.vector.tensor_copy(b_tile[:], b_bank[:])

        sums = [psum.tile([P, N], F32, name=f"sums{i}") for i in range(H // P)]
        for i in range(H // P):
            for k in range(K // P):
                nc.tensor.matmul(
                    sums[i][:], w_tile[:, k, i * P : (i + 1) * P], x_tile[:, k, :], start=k == 0, stop=k == K // P - 1
                )

        c_bank = psum.tile([P, N], F32)
        nc.tensor.matmul(c_bank[:], ones_row[:], c_row[:], start=True, stop=True)

        relu0 = held.tile([P, N], F32)
        nc.vector.tensor_scalar(relu0[:], sums[0][:], b_tile[:, 0:1], 0.0, op0=ADD, op1=MAX)
        relu1 = held.tile([P, N], F32)
        nc.scalar.activation(relu1[:], sums[1][:], RELU, bias=b_tile[:, 1:2])
        hidden = [held.tile([P, N], BF16, name=f"hidden{i}") for i in range(H // P)]
        nc.vector.tensor_tensor(hidden[0][:], relu0[:], c_bank[:], MULT)
        nc.vector.tensor_tensor(hidden[1][:], relu1[:], c_bank[:], MULT)

        windows = [psum.tile([P, S], F32, name=f"window{m}") for m in range(M // P)]
        for m in range(M // P):
            nc.tensor.matmul(windows[m][:], ident[:], base_tile[:, m, :], start=True, stop=False)

        for m in range(M // P):
            for i in range(H // P):
                nc.tensor.matmul(
                    windows[m][:].indirect(offsets[:]),
                    w2_tile[:, i, m * P : (m + 1) * P],
                    hidden[i][:],
                    start=False,
                    stop=i == H // P - 1,
                )

        out_tiles = [held.tile([P, S], F32, name=f"out{m}") for m in range(M // P)]
        nc.scalar.copy(out_tiles[0][:], windows[0][:])
        nc.sync.dma_start(out[0:P, :], out_tiles[0][:])
        nc.vector.tensor_copy(out_tiles[1][:], windows[1][:])
        nc.sync.dma_start(out[P : 2 * P, :], out_tiles[1][:])
